import numpy as np, ml_dtypes
CORES = [23,119,17,113]
N = 4
R = 256
def setup_inputs(rng):
    m = (rng.standard_normal((N, 128, 128), dtype=np.float32) / 11).astype(ml_dtypes.bfloat16)
    q = rng.standard_normal((128, R), dtype=np.float32).astype(ml_dtypes.bfloat16)
    return {"m": m, "mt": m.transpose(0, 2, 1).copy(), "q": np.broadcast_to(q, (N, 128, R)).copy()}
def setup_inputs_big(rng):
    d = setup_inputs(rng)
    for k in ("m", "mt", "q"): d[k] = (d[k].astype(np.float32) * 1024.0).astype(d[k].dtype)
    return d
def setup_inputs_small(rng):
    d = setup_inputs(rng)
    for k in ("m", "mt", "q"): d[k] = (d[k].astype(np.float32) * (1 / 1024.0)).astype(d[k].dtype)
    return d
def setup_inputs_apart(rng):
    d = setup_inputs(rng)
    f = (10.0 ** rng.permutation(np.linspace(-1.5, 1.5, N))).astype(np.float32).reshape(N, 1, 1)
    for k in ("m", "mt"): d[k] = (d[k].astype(np.float32) * f).astype(d[k].dtype)
    return d
def tie_inputs(x):
    x = dict(x)
    x["mt"] = x["m"].transpose(0, 2, 1).copy(); x["q"] = np.broadcast_to(x["q"][0], x["q"].shape).copy()
    return x
def reference(m, mt, q):
    M, MT, Q = m.astype(np.float64), mt.astype(np.float64), q.astype(np.float64)
    p = sum(MT[j].T @ Q[j] for j in range(N))
    q2 = sum(M[j].T @ p for j in range(N))
    return {"p": np.broadcast_to(p.astype(ml_dtypes.bfloat16 if m.dtype != np.float64 else np.float64), (N, 128, R)), "q2": np.broadcast_to(q2.astype(ml_dtypes.bfloat16 if m.dtype != np.float64 else np.float64), (N, 128, R))}

@@ -1,0 +1,135 @@
+from concourse.bass import DstId, RemoteDMATransfer
+
+N = 4
+D = 128
+R = 256
+H = R // 2
+
+SCRATCH = {
+    "mts": ("sbuf", [128, N * D], "bfloat16"),
+    "qs": ("sbuf", [128, R], "bfloat16"),
+    "zs": ("sbuf", [128, D + 1], "bfloat16"),
+    "zd": ("dram", [D + 1, 128], "bfloat16"),
+    "eye": ("sbuf", [128, D], "bfloat16"),
+    "ss": ("sbuf", [128, D], "bfloat16"),
+    "ps": ("sbuf", [128, R], "bfloat16"),
+    "q2s": ("sbuf", [128, R], "bfloat16"),
+    "acc_s": ("psum", [128, 512], "float32"),
+    "acc_pa": ("psum", [128, 512], "float32"),
+    "acc_pb": ("psum", [128, 512], "float32"),
+    "acc_qa": ("psum", [128, 512], "float32"),
+    "acc_qb": ("psum", [128, 512], "float32"),
+}
+SEMAPHORES = ["ld_mt", "ld_q", "fill", "zout", "eye_in", "sent", "arr0", "arr1", "arr2", "arr3",
+              "mm_s", "mm_pa", "mm_pb", "mm_qa", "mm_qb", "cp_s", "cp_pa", "cp_pb", "cp_q", "st_p", "st_q"]
+
+
+def _engines(mask):
+    return [e for e in range(mask.bit_length()) if (mask >> e) & 1]
+
+
+def _bits(es):
+    m = 0
+    for e in es:
+        m |= 1 << e
+    return m
+
+
+def _plan(core, cores, topo):
+    far = [c for c in cores if c != core and topo.chip(c) != topo.chip(core)]
+    near = [c for c in cores if c != core and topo.chip(c) == topo.chip(core)]
+    plan, used = {}, []
+    for i, c in enumerate(far):
+        es = _engines(topo.mask(core, c))
+        k = len(es) // len(far)
+        plan[c] = es[i * k:(i + 1) * k]
+        used += plan[c]
+    for i, c in enumerate(near):
+        es = [e for e in _engines(topo.mask(core, c)) if e not in used]
+        k = len(es) // len(near)
+        plan[c] = es[i * k:(i + 1) * k]
+    return far, near, plan
+
+
+def rank_program(g, core, T, topo):
+    rank = T.rank_of(core)
+    if rank is None:
+        return
+    S = T.sem
+    te, ve, sy, sc = g.tensor, g.vector, g.sync, g.scalar
+    far, near, plan = _plan(core, T.cores, topo)
+
+    def slot(j):
+        return T.mts[:, j * D:(j + 1) * D]
+
+    sy.dma_start(slot(rank), T.mt[:, :]).then_inc(S.ld_mt, 16)
+    sy.dma_start(T.qs[:, :], T.q[:, :]).then_inc(S.ld_q, 16)
+
+    ve.memset(T.zs[:, 0:1], 1.0).then_inc(S.fill, 1)
+    ve.memset(T.zs[:, 1:D + 1], 0.0).then_inc(S.fill, 1)
+    sc.wait_ge(S.fill, 2)
+    sc.dma_start(T.zd[:, :], T.zs[:, :]).then_inc(S.zout, 16)
+    sc.wait_ge(S.zout, 16)
+    sc.dma_start(T.eye[:, :], T.zd[0:D, :]).then_inc(S.eye_in, 16)
+
+    mine = S["arr%d" % rank]
+    g.wait_ge(S.ld_mt, 16)
+    trs = []
+    for c in far:
+        rid, pid, _ = topo.addr(c)
+        trs.append(RemoteDMATransfer(dst_ids=[DstId(rid=rid, pnc=pid)], dma_engine_mask=_bits(plan[c]),
+                                     remote_sem=mine, src=slot(rank), dst=slot(rank)))
+    g.remote_dma_fused(trs, local_sem=S.sent)
+    for c in near:
+        rid, pid, _ = topo.addr(c)
+        g.remote_dma(slot(rank), slot(rank), mine, S.sent, pid, rid, _bits(plan[c]))
+
+    qa, qb = T.qs[:, 0:H], T.qs[:, H:R]
+    order = [core] + near + far
+    for i, c in enumerate(order):
+        j = T.rank_of(c)
+        first, last = i == 0, i == len(order) - 1
+        if first:
+            te.wait_ge(S.ld_mt, 16)
+            te.wait_ge(S.ld_q, 16)
+            te.matmul(T.acc_pa[:, 0:H], slot(j), qa, True, False)
+            te.matmul(T.acc_pb[:, 0:H], slot(j), qb, True, False)
+            te.wait_ge(S.eye_in, 16)
+            te.matmul(T.acc_s[:, 0:D], slot(j), T.eye[:, :], True, False)
+            continue
+        te.wait_ge(S["arr%d" % j], len(_plan(c, T.cores, topo)[2][core]))
+        a = te.matmul(T.acc_s[:, 0:D], slot(j), T.eye[:, :], False, last)
+        b = te.matmul(T.acc_pa[:, 0:H], slot(j), qa, False, last)
+        d = te.matmul(T.acc_pb[:, 0:H], slot(j), qb, False, last)
+        if last:
+            a.then_inc(S.mm_s, 1)
+            b.then_inc(S.mm_pa, 1)
+            d.then_inc(S.mm_pb, 1)
+
+    ve.wait_ge(S.mm_s, 1)
+    ve.tensor_copy(T.ss[:, :], T.acc_s[:, 0:D]).then_inc(S.cp_s, 1)
+    ve.wait_ge(S.mm_pa, 1)
+    ve.tensor_copy(T.ps[:, 0:H], T.acc_pa[:, 0:H]).then_inc(S.cp_pa, 1)
+    ve.wait_ge(S.mm_pb, 1)
+    ve.tensor_copy(T.ps[:, H:R], T.acc_pb[:, 0:H]).then_inc(S.cp_pb, 1)
+
+    te.wait_ge(S.cp_s, 1)
+    te.wait_ge(S.cp_pa, 1)
+    te.matmul(T.acc_qa[:, 0:H], T.ss[:, :], T.ps[:, 0:H], True, True).then_inc(S.mm_qa, 1)
+    te.wait_ge(S.cp_pb, 1)
+    te.matmul(T.acc_qb[:, 0:H], T.ss[:, :], T.ps[:, H:R], True, True).then_inc(S.mm_qb, 1)
+
+    ve.wait_ge(S.mm_qa, 1)
+    ve.tensor_copy(T.q2s[:, 0:H], T.acc_qa[:, 0:H]).then_inc(S.cp_q, 1)
+    ve.wait_ge(S.mm_qb, 1)
+    ve.tensor_copy(T.q2s[:, H:R], T.acc_qb[:, 0:H]).then_inc(S.cp_q, 1)
+
+    sy.wait_ge(S.cp_pa, 1)
+    sy.wait_ge(S.cp_pb, 1)
+    sy.dma_start(T.p[:, :], T.ps[:, :]).then_inc(S.st_p, 16)
+    sc.wait_ge(S.cp_q, 2)
+    sc.dma_start(T.q2[:, :], T.q2s[:, :]).then_inc(S.st_q, 16)
+
+    g.wait_ge(S.sent, sum(len(plan[c]) for c in far + near))
+    sy.wait_ge(S.st_p, 16)
+    sc.wait_ge(S.st_q, 16)

@@ -1,16 +1,20 @@
 from concourse.bass import DstId, RemoteDMATransfer
+from concourse.mybir import AluOpType
 
 N = 4
 D = 128
 R = 256
 H = R // 2
+B = D // 2
 
 SCRATCH = {
     "mts": ("sbuf", [128, N * D], "bfloat16"),
     "qs": ("sbuf", [128, R], "bfloat16"),
-    "zs": ("sbuf", [128, D + 1], "bfloat16"),
-    "zd": ("dram", [D + 1, 128], "bfloat16"),
+    "zs": ("sbuf", [128, B + 1], "bfloat16"),
+    "zd": ("dram", [128, B + 1], "bfloat16"),
     "eye": ("sbuf", [128, D], "bfloat16"),
+    "t1": ("sbuf", [128, D], "bfloat16"),
+    "tf": ("sbuf", [128, D], "bfloat16"),
     "ss": ("sbuf", [128, D], "bfloat16"),
     "ps": ("sbuf", [128, R], "bfloat16"),
     "q2s": ("sbuf", [128, R], "bfloat16"),
@@ -20,7 +24,8 @@ SCRATCH = {
     "acc_qa": ("psum", [128, 512], "float32"),
     "acc_qb": ("psum", [128, 512], "float32"),
 }
-SEMAPHORES = ["ld_mt", "ld_q", "fill", "zout", "eye_in", "sent", "arr0", "arr1", "arr2", "arr3",
+SEMAPHORES = ["ld_mt", "ld_q", "fill", "fill_e", "tab", "eye_in", "sent", "sum1", "sum2",
+              "arr0", "arr1", "arr2", "arr3",
               "mm_s", "mm_pa", "mm_pb", "mm_qa", "mm_qb", "cp_s", "cp_pa", "cp_pb", "cp_q", "st_p", "st_q"]
 
 
@@ -48,7 +53,7 @@ def _plan(core, cores, topo):
         es = [e for e in _engines(topo.mask(core, c)) if e not in used]
         k = len(es) // len(near)
         plan[c] = es[i * k:(i + 1) * k]
-    return far, near, plan
+    return far, near, plan, used
 
 
 def rank_program(g, core, T, topo):
@@ -57,20 +62,28 @@ def rank_program(g, core, T, topo):
         return
     S = T.sem
     te, ve, sy, sc = g.tensor, g.vector, g.sync, g.scalar
-    far, near, plan = _plan(core, T.cores, topo)
+    far, near, plan, used = _plan(core, T.cores, topo)
+    twin = [c for c in far if topo.die(c) == topo.die(core)][0]
 
     def slot(j):
         return T.mts[:, j * D:(j + 1) * D]
 
+    def landed(c):
+        return S["arr%d" % T.rank_of(c)], len(_plan(c, T.cores, topo)[2][core])
+
     sy.dma_start(slot(rank), T.mt[:, :]).then_inc(S.ld_mt, 16)
     sy.dma_start(T.qs[:, :], T.q[:, :]).then_inc(S.ld_q, 16)
 
-    ve.memset(T.zs[:, 0:1], 1.0).then_inc(S.fill, 1)
-    ve.memset(T.zs[:, 1:D + 1], 0.0).then_inc(S.fill, 1)
-    sc.wait_ge(S.fill, 2)
-    sc.dma_start(T.zd[:, :], T.zs[:, :]).then_inc(S.zout, 16)
-    sc.wait_ge(S.zout, 16)
-    sc.dma_start(T.eye[:, :], T.zd[0:D, :]).then_inc(S.eye_in, 16)
+    ve.memset(T.zs[0:B, 0:1], 1.0).then_inc(S.fill, 1)
+    ve.memset(T.zs[0:B, 1:B + 1], 0.0).then_inc(S.fill, 1)
+    ve.memset(T.zs[B:D, 0:B], 0.0).then_inc(S.fill, 1)
+    ve.memset(T.zs[B:D, B:B + 1], 1.0).then_inc(S.fill, 1)
+    ve.memset(T.eye[B:D, 0:B], 0.0).then_inc(S.fill_e, 1)
+    ve.memset(T.eye[0:B, B:D], 0.0).then_inc(S.fill_e, 1)
+
+    g.wait_ge(S.fill, 4)
+    rid, pid, _ = topo.addr(twin)
+    g.remote_dma(T.zd[:, :], T.zs[:, :], S.tab, S.sent, pid, rid, _bits(used))
 
     mine = S["arr%d" % rank]
     g.wait_ge(S.ld_mt, 16)
@@ -84,6 +97,14 @@ def rank_program(g, core, T, topo):
         rid, pid, _ = topo.addr(c)
         g.remote_dma(slot(rank), slot(rank), mine, S.sent, pid, rid, _bits(plan[c]))
 
+    ntab = len(_plan(twin, T.cores, topo)[3])
+    sc.wait_ge(S.fill_e, 2)
+    sc.wait_ge(S.tab, ntab)
+    sc.dma_start(T.eye[0:B + 1, 0:B], T.zd[0:B, :]).then_inc(S.eye_in, 16)
+    sy.wait_ge(S.fill_e, 2)
+    sy.wait_ge(S.tab, ntab)
+    sy.dma_start(T.eye[B - 1:D, B:D], T.zd[B:D, :]).then_inc(S.eye_in, 16)
+
     qa, qb = T.qs[:, 0:H], T.qs[:, H:R]
     order = [core] + near + far
     for i, c in enumerate(order):
@@ -92,26 +113,32 @@ def rank_program(g, core, T, topo):
         if first:
             te.wait_ge(S.ld_mt, 16)
             te.wait_ge(S.ld_q, 16)
-            te.matmul(T.acc_pa[:, 0:H], slot(j), qa, True, False)
-            te.matmul(T.acc_pb[:, 0:H], slot(j), qb, True, False)
-            te.wait_ge(S.eye_in, 16)
-            te.matmul(T.acc_s[:, 0:D], slot(j), T.eye[:, :], True, False)
-            continue
-        te.wait_ge(S["arr%d" % j], len(_plan(c, T.cores, topo)[2][core]))
-        a = te.matmul(T.acc_s[:, 0:D], slot(j), T.eye[:, :], False, last)
-        b = te.matmul(T.acc_pa[:, 0:H], slot(j), qa, False, last)
-        d = te.matmul(T.acc_pb[:, 0:H], slot(j), qb, False, last)
+        else:
+            te.wait_ge(*landed(c))
+        b = te.matmul(T.acc_pa[:, 0:H], slot(j), qa, first, last)
+        d = te.matmul(T.acc_pb[:, 0:H], slot(j), qb, first, last)
         if last:
-            a.then_inc(S.mm_s, 1)
             b.then_inc(S.mm_pa, 1)
             d.then_inc(S.mm_pb, 1)
+    te.wait_ge(S.eye_in, 32)
+    te.wait_ge(S.sum1, 1)
+    te.matmul(T.acc_s[:, 0:D], T.t1[:, :], T.eye[:, :], True, False)
+    te.wait_ge(S.sum2, 1)
+    te.matmul(T.acc_s[:, 0:D], T.tf[:, :], T.eye[:, :], False, True).then_inc(S.mm_s, 1)
 
-    ve.wait_ge(S.mm_s, 1)
-    ve.tensor_copy(T.ss[:, :], T.acc_s[:, 0:D]).then_inc(S.cp_s, 1)
+    ve.wait_ge(S.ld_mt, 16)
+    ve.wait_ge(*landed(near[0]))
+    ve.tensor_tensor(T.t1[:, :], slot(rank), slot(T.rank_of(near[0])), AluOpType.add).then_inc(S.sum1, 1)
+    ve.wait_ge(*landed(far[0]))
+    ve.wait_ge(*landed(far[1]))
+    ve.tensor_tensor(T.tf[:, :], slot(T.rank_of(far[0])), slot(T.rank_of(far[1])), AluOpType.add).then_inc(S.sum2, 1)
+
     ve.wait_ge(S.mm_pa, 1)
     ve.tensor_copy(T.ps[:, 0:H], T.acc_pa[:, 0:H]).then_inc(S.cp_pa, 1)
     ve.wait_ge(S.mm_pb, 1)
     ve.tensor_copy(T.ps[:, H:R], T.acc_pb[:, 0:H]).then_inc(S.cp_pb, 1)
+    ve.wait_ge(S.mm_s, 1)
+    ve.tensor_copy(T.ss[:, :], T.acc_s[:, 0:D]).then_inc(S.cp_s, 1)
 
     te.wait_ge(S.cp_s, 1)
     te.wait_ge(S.cp_pa, 1)
@@ -130,6 +157,6 @@ def rank_program(g, core, T, topo):
     sc.wait_ge(S.cp_q, 2)
     sc.dma_start(T.q2[:, :], T.q2s[:, :]).then_inc(S.st_q, 16)
 
-    g.wait_ge(S.sent, sum(len(plan[c]) for c in far + near))
+    g.wait_ge(S.sent, sum(len(plan[c]) for c in far + near) + len(used))
     sy.wait_ge(S.st_p, 16)
     sc.wait_ge(S.st_q, 16)

@@ -1,32 +1,38 @@
 from concourse.bass import DstId, RemoteDMATransfer
-from concourse.mybir import AluOpType
+from concourse.mybir import AluOpType, ActivationFunctionType
 
 N = 4
 D = 128
 R = 256
 H = R // 2
-B = D // 2
+C = R // 4
+W = 8
 
 SCRATCH = {
     "mts": ("sbuf", [128, N * D], "bfloat16"),
+    "ms": ("sbuf", [128, D], "bfloat16"),
     "qs": ("sbuf", [128, R], "bfloat16"),
-    "zs": ("sbuf", [128, B + 1], "bfloat16"),
-    "zd": ("dram", [128, B + 1], "bfloat16"),
+    "pi": ("sbuf", [128, W], "bfloat16"),
+    "pr": ("sbuf", [128, W], "bfloat16"),
+    "one": ("sbuf", [128, D], "bfloat16"),
+    "col": ("sbuf", [128, D], "bfloat16"),
     "eye": ("sbuf", [128, D], "bfloat16"),
-    "t1": ("sbuf", [128, D], "bfloat16"),
-    "tf": ("sbuf", [128, D], "bfloat16"),
     "ss": ("sbuf", [128, D], "bfloat16"),
     "ps": ("sbuf", [128, R], "bfloat16"),
     "q2s": ("sbuf", [128, R], "bfloat16"),
     "acc_s": ("psum", [128, 512], "float32"),
-    "acc_pa": ("psum", [128, 512], "float32"),
-    "acc_pb": ("psum", [128, 512], "float32"),
+    "acc_p0": ("psum", [128, 512], "float32"),
+    "acc_p1": ("psum", [128, 512], "float32"),
+    "acc_p2": ("psum", [128, 512], "float32"),
+    "acc_p3": ("psum", [128, 512], "float32"),
     "acc_qa": ("psum", [128, 512], "float32"),
     "acc_qb": ("psum", [128, 512], "float32"),
+    "acc_qc": ("psum", [128, 512], "float32"),
 }
-SEMAPHORES = ["ld_mt", "ld_q", "fill", "fill_e", "tab", "eye_in", "sent", "sum1", "sum2",
+SEMAPHORES = ["ld_mt", "ld_q", "ld_m", "numb", "fill", "scan", "tab", "eye_ok", "sent",
               "arr0", "arr1", "arr2", "arr3",
-              "mm_s", "mm_pa", "mm_pb", "mm_qa", "mm_qb", "cp_s", "cp_pa", "cp_pb", "cp_q", "st_p", "st_q"]
+              "mm_s", "mm_p0", "mm_p1", "mm_p2", "mm_p3", "mm_qa", "mm_qb", "mm_qc",
+              "cp_s", "cp_p0", "cp_p1", "cp_p2", "cp_p3", "cp_qa", "cp_qb", "cp_qc", "st_p", "st_q"]
 
 
 def _engines(mask):
@@ -40,20 +46,14 @@ def _bits(es):
     return m
 
 
-def _plan(core, cores, topo):
+def _peers(core, cores, topo):
     far = [c for c in cores if c != core and topo.chip(c) != topo.chip(core)]
-    near = [c for c in cores if c != core and topo.chip(c) == topo.chip(core)]
-    plan, used = {}, []
-    for i, c in enumerate(far):
-        es = _engines(topo.mask(core, c))
-        k = len(es) // len(far)
-        plan[c] = es[i * k:(i + 1) * k]
-        used += plan[c]
-    for i, c in enumerate(near):
-        es = [e for e in _engines(topo.mask(core, c)) if e not in used]
-        k = len(es) // len(near)
-        plan[c] = es[i * k:(i + 1) * k]
-    return far, near, plan, used
+    near = [c for c in cores if c != core and topo.chip(c) == topo.chip(core)][0]
+    twin = [c for c in far if topo.die(c) == topo.die(core)][0]
+    cross = [c for c in far if c != twin][0]
+    off = _engines(topo.mask(core, twin))
+    on = [e for e in _engines(topo.mask(core, near)) if e not in off]
+    return twin, cross, near, off, on
 
 
 def rank_program(g, core, T, topo):
@@ -62,101 +62,104 @@ def rank_program(g, core, T, topo):
         return
     S = T.sem
     te, ve, sy, sc = g.tensor, g.vector, g.sync, g.scalar
-    far, near, plan, used = _plan(core, T.cores, topo)
-    twin = [c for c in far if topo.die(c) == topo.die(core)][0]
+    twin, cross, near, off, on = _peers(core, T.cores, topo)
 
-    def slot(j):
+    def slot(c):
+        j = T.rank_of(c)
         return T.mts[:, j * D:(j + 1) * D]
 
     def landed(c):
-        return S["arr%d" % T.rank_of(c)], len(_plan(c, T.cores, topo)[2][core])
+        p = _peers(c, T.cores, topo)
+        return S["arr%d" % T.rank_of(c)], len(p[4] if c == near else p[3])
 
-    sy.dma_start(slot(rank), T.mt[:, :]).then_inc(S.ld_mt, 16)
+    def send(c, dst, src, sem, es):
+        rid, pid, _ = topo.addr(c)
+        g.remote_dma(dst, src, sem, S.sent, pid, rid, _bits(es))
+
+    sy.dma_start(slot(core), T.mt[:, :]).then_inc(S.ld_mt, 16)
     sy.dma_start(T.qs[:, :], T.q[:, :]).then_inc(S.ld_q, 16)
+    sy.dma_start(T.ms[:, :], T.m[:, :]).then_inc(S.ld_m, 16)
 
-    ve.memset(T.zs[0:B, 0:1], 1.0).then_inc(S.fill, 1)
-    ve.memset(T.zs[0:B, 1:B + 1], 0.0).then_inc(S.fill, 1)
-    ve.memset(T.zs[B:D, 0:B], 0.0).then_inc(S.fill, 1)
-    ve.memset(T.zs[B:D, B:B + 1], 1.0).then_inc(S.fill, 1)
-    ve.memset(T.eye[B:D, 0:B], 0.0).then_inc(S.fill_e, 1)
-    ve.memset(T.eye[0:B, B:D], 0.0).then_inc(S.fill_e, 1)
-
-    g.wait_ge(S.fill, 4)
-    rid, pid, _ = topo.addr(twin)
-    g.remote_dma(T.zd[:, :], T.zs[:, :], S.tab, S.sent, pid, rid, _bits(used))
+    g.iota(T.pi[:, :], [[0, W]], 1, 1, allow_small_or_imprecise_dtypes=True).then_inc(S.numb, 1)
+    g.wait_ge(S.numb, 1)
+    send(twin, T.pr[:, :], T.pi[:, :], S.tab, off)
 
     mine = S["arr%d" % rank]
     g.wait_ge(S.ld_mt, 16)
-    trs = []
-    for c in far:
-        rid, pid, _ = topo.addr(c)
-        trs.append(RemoteDMATransfer(dst_ids=[DstId(rid=rid, pnc=pid)], dma_engine_mask=_bits(plan[c]),
-                                     remote_sem=mine, src=slot(rank), dst=slot(rank)))
-    g.remote_dma_fused(trs, local_sem=S.sent)
-    for c in near:
-        rid, pid, _ = topo.addr(c)
-        g.remote_dma(slot(rank), slot(rank), mine, S.sent, pid, rid, _bits(plan[c]))
+    send(twin, slot(core), slot(core), mine, off)
+    send(cross, slot(core), slot(core), mine, off)
+    send(near, slot(core), slot(core), mine, on)
 
-    ntab = len(_plan(twin, T.cores, topo)[3])
-    sc.wait_ge(S.fill_e, 2)
-    sc.wait_ge(S.tab, ntab)
-    sc.dma_start(T.eye[0:B + 1, 0:B], T.zd[0:B, :]).then_inc(S.eye_in, 16)
-    sy.wait_ge(S.fill_e, 2)
-    sy.wait_ge(S.tab, ntab)
-    sy.dma_start(T.eye[B - 1:D, B:D], T.zd[B:D, :]).then_inc(S.eye_in, 16)
+    ve.memset(T.one[:, :], 1.0).then_inc(S.fill, 1)
+    ve.wait_ge(S.fill, 1)
+    ve.tensor_tensor_scan(T.col[:, :], T.one[:, :], T.one[:, :], 0.0, AluOpType.mult, AluOpType.add).then_inc(S.scan, 1)
+    ve.wait_ge(S.scan, 1)
+    ve.wait_ge(S.tab, len(_peers(twin, T.cores, topo)[3]))
+    ve.tensor_scalar(T.eye[:, :], T.col[:, :], T.pr[:, 0:1], None, AluOpType.is_equal).then_inc(S.eye_ok, 1)
 
-    qa, qb = T.qs[:, 0:H], T.qs[:, H:R]
-    order = [core] + near + far
-    for i, c in enumerate(order):
-        j = T.rank_of(c)
-        first, last = i == 0, i == len(order) - 1
-        if first:
-            te.wait_ge(S.ld_mt, 16)
-            te.wait_ge(S.ld_q, 16)
-        else:
-            te.wait_ge(*landed(c))
-        b = te.matmul(T.acc_pa[:, 0:H], slot(j), qa, first, last)
-        d = te.matmul(T.acc_pb[:, 0:H], slot(j), qb, first, last)
+    accp = [T.acc_p0, T.acc_p1, T.acc_p2, T.acc_p3]
+
+    def p_part(c, first, last):
+        for k in range(4):
+            i = te.matmul(accp[k][:, 0:C], slot(c), T.qs[:, k * C:(k + 1) * C], first, last)
+            if last:
+                i.then_inc(S["mm_p%d" % k], 1)
+
+    def s_part(c, first, last):
+        i = te.matmul(T.acc_s[:, 0:D], slot(c), T.eye[:, :], first, last)
         if last:
-            b.then_inc(S.mm_pa, 1)
-            d.then_inc(S.mm_pb, 1)
-    te.wait_ge(S.eye_in, 32)
-    te.wait_ge(S.sum1, 1)
-    te.matmul(T.acc_s[:, 0:D], T.t1[:, :], T.eye[:, :], True, False)
-    te.wait_ge(S.sum2, 1)
-    te.matmul(T.acc_s[:, 0:D], T.tf[:, :], T.eye[:, :], False, True).then_inc(S.mm_s, 1)
+            i.then_inc(S.mm_s, 1)
 
-    ve.wait_ge(S.ld_mt, 16)
-    ve.wait_ge(*landed(near[0]))
-    ve.tensor_tensor(T.t1[:, :], slot(rank), slot(T.rank_of(near[0])), AluOpType.add).then_inc(S.sum1, 1)
-    ve.wait_ge(*landed(far[0]))
-    ve.wait_ge(*landed(far[1]))
-    ve.tensor_tensor(T.tf[:, :], slot(T.rank_of(far[0])), slot(T.rank_of(far[1])), AluOpType.add).then_inc(S.sum2, 1)
+    te.wait_ge(S.ld_mt, 16)
+    te.wait_ge(S.ld_q, 16)
+    p_part(core, True, False)
+    te.wait_ge(*landed(twin))
+    p_part(twin, False, False)
+    te.wait_ge(S.eye_ok, 1)
+    s_part(twin, True, False)
+    te.wait_ge(*landed(near))
+    s_part(near, False, False)
+    p_part(near, False, False)
+    te.wait_ge(*landed(cross))
+    s_part(cross, False, True)
+    p_part(cross, False, True)
 
-    ve.wait_ge(S.mm_pa, 1)
-    ve.tensor_copy(T.ps[:, 0:H], T.acc_pa[:, 0:H]).then_inc(S.cp_pa, 1)
-    ve.wait_ge(S.mm_pb, 1)
-    ve.tensor_copy(T.ps[:, H:R], T.acc_pb[:, 0:H]).then_inc(S.cp_pb, 1)
+    ve.wait_ge(S.ld_m, 16)
     ve.wait_ge(S.mm_s, 1)
-    ve.tensor_copy(T.ss[:, :], T.acc_s[:, 0:D]).then_inc(S.cp_s, 1)
+    ve.tensor_tensor(T.ss[:, :], T.acc_s[:, 0:D], T.ms[:, :], AluOpType.add).then_inc(S.cp_s, 1)
+    for k in range(4):
+        q = sc if k % 2 == 0 else ve
+        q.wait_ge(S["mm_p%d" % k], 1)
+        if k % 2 == 0:
+            i = sc.activation(T.ps[:, k * C:(k + 1) * C], accp[k][:, 0:C], ActivationFunctionType.Copy)
+        else:
+            i = ve.tensor_copy(T.ps[:, k * C:(k + 1) * C], accp[k][:, 0:C])
+        i.then_inc(S["cp_p%d" % k], 1)
 
     te.wait_ge(S.cp_s, 1)
-    te.wait_ge(S.cp_pa, 1)
+    te.wait_ge(S.cp_p0, 1)
+    te.wait_ge(S.cp_p1, 1)
     te.matmul(T.acc_qa[:, 0:H], T.ss[:, :], T.ps[:, 0:H], True, True).then_inc(S.mm_qa, 1)
-    te.wait_ge(S.cp_pb, 1)
-    te.matmul(T.acc_qb[:, 0:H], T.ss[:, :], T.ps[:, H:R], True, True).then_inc(S.mm_qb, 1)
+    te.wait_ge(S.cp_p2, 1)
+    te.matmul(T.acc_qb[:, 0:C], T.ss[:, :], T.ps[:, H:H + C], True, True).then_inc(S.mm_qb, 1)
+    te.wait_ge(S.cp_p3, 1)
+    te.matmul(T.acc_qc[:, 0:C], T.ss[:, :], T.ps[:, H + C:R], True, True).then_inc(S.mm_qc, 1)
 
     ve.wait_ge(S.mm_qa, 1)
-    ve.tensor_copy(T.q2s[:, 0:H], T.acc_qa[:, 0:H]).then_inc(S.cp_q, 1)
-    ve.wait_ge(S.mm_qb, 1)
-    ve.tensor_copy(T.q2s[:, H:R], T.acc_qb[:, 0:H]).then_inc(S.cp_q, 1)
+    ve.tensor_copy(T.q2s[:, 0:H], T.acc_qa[:, 0:H]).then_inc(S.cp_qa, 1)
+    sc.wait_ge(S.mm_qb, 1)
+    sc.activation(T.q2s[:, H:H + C], T.acc_qb[:, 0:C], ActivationFunctionType.Copy).then_inc(S.cp_qb, 1)
+    sc.wait_ge(S.mm_qc, 1)
+    sc.activation(T.q2s[:, H + C:R], T.acc_qc[:, 0:C], ActivationFunctionType.Copy).then_inc(S.cp_qc, 1)
 
-    sy.wait_ge(S.cp_pa, 1)
-    sy.wait_ge(S.cp_pb, 1)
+    for k in range(4):
+        sy.wait_ge(S["cp_p%d" % k], 1)
     sy.dma_start(T.p[:, :], T.ps[:, :]).then_inc(S.st_p, 16)
-    sc.wait_ge(S.cp_q, 2)
+    sc.wait_ge(S.cp_qa, 1)
+    sc.wait_ge(S.cp_qb, 1)
+    sc.wait_ge(S.cp_qc, 1)
     sc.dma_start(T.q2[:, :], T.q2s[:, :]).then_inc(S.st_q, 16)
 
-    g.wait_ge(S.sent, sum(len(plan[c]) for c in far + near) + len(used))
+    g.wait_ge(S.sent, 3 * len(off) + len(on))
     sy.wait_ge(S.st_p, 16)
     sc.wait_ge(S.st_q, 16)

from concourse.bass import DstId, RemoteDMATransfer
from concourse.mybir import AluOpType, ActivationFunctionType

N = 4
D = 128
R = 256
H = R // 2
C = R // 4
W = 8

SCRATCH = {
    "mts": ("sbuf", [128, N * D], "bfloat16"),
    "ms": ("sbuf", [128, D], "bfloat16"),
    "qs": ("sbuf", [128, R], "bfloat16"),
    "pi": ("sbuf", [128, W], "bfloat16"),
    "pr": ("sbuf", [128, W], "bfloat16"),
    "one": ("sbuf", [128, D], "bfloat16"),
    "col": ("sbuf", [128, D], "bfloat16"),
    "eye": ("sbuf", [128, D], "bfloat16"),
    "ss": ("sbuf", [128, D], "bfloat16"),
    "ps": ("sbuf", [128, R], "bfloat16"),
    "q2s": ("sbuf", [128, R], "bfloat16"),
    "acc_s": ("psum", [128, 512], "float32"),
    "acc_p0": ("psum", [128, 512], "float32"),
    "acc_p1": ("psum", [128, 512], "float32"),
    "acc_p2": ("psum", [128, 512], "float32"),
    "acc_p3": ("psum", [128, 512], "float32"),
    "acc_qa": ("psum", [128, 512], "float32"),
    "acc_qb": ("psum", [128, 512], "float32"),
    "acc_qc": ("psum", [128, 512], "float32"),
}
SEMAPHORES = ["ld_mt", "ld_q", "ld_m", "numb", "fill", "scan", "tab", "eye_ok", "sent",
              "arr0", "arr1", "arr2", "arr3",
              "mm_s", "mm_p0", "mm_p1", "mm_p2", "mm_p3", "mm_qa", "mm_qb", "mm_qc",
              "cp_s", "cp_p0", "cp_p1", "cp_p2", "cp_p3", "cp_qa", "cp_qb", "cp_qc", "st_p", "st_q"]


def _engines(mask):
    return [e for e in range(mask.bit_length()) if (mask >> e) & 1]


def _bits(es):
    m = 0
    for e in es:
        m |= 1 << e
    return m


def _peers(core, cores, topo):
    far = [c for c in cores if c != core and topo.chip(c) != topo.chip(core)]
    near = [c for c in cores if c != core and topo.chip(c) == topo.chip(core)][0]
    twin = [c for c in far if topo.die(c) == topo.die(core)][0]
    cross = [c for c in far if c != twin][0]
    off = _engines(topo.mask(core, twin))
    on = [e for e in _engines(topo.mask(core, near)) if e not in off]
    return twin, cross, near, off, on


def rank_program(g, core, T, topo):
    rank = T.rank_of(core)
    if rank is None:
        return
    S = T.sem
    te, ve, sy, sc = g.tensor, g.vector, g.sync, g.scalar
    twin, cross, near, off, on = _peers(core, T.cores, topo)

    def slot(c):
        j = T.rank_of(c)
        return T.mts[:, j * D:(j + 1) * D]

    def landed(c):
        p = _peers(c, T.cores, topo)
        return S["arr%d" % T.rank_of(c)], len(p[4] if c == near else p[3])

    def send(c, dst, src, sem, es):
        rid, pid, _ = topo.addr(c)
        g.remote_dma(dst, src, sem, S.sent, pid, rid, _bits(es))

    sy.dma_start(slot(core), T.mt[:, :]).then_inc(S.ld_mt, 16)
    sy.dma_start(T.qs[:, :], T.q[:, :]).then_inc(S.ld_q, 16)
    sy.dma_start(T.ms[:, :], T.m[:, :]).then_inc(S.ld_m, 16)

    g.iota(T.pi[:, :], [[0, W]], 1, 1, allow_small_or_imprecise_dtypes=True).then_inc(S.numb, 1)
    g.wait_ge(S.numb, 1)
    send(twin, T.pr[:, :], T.pi[:, :], S.tab, off)

    mine = S["arr%d" % rank]
    g.wait_ge(S.ld_mt, 16)
    send(twin, slot(core), slot(core), mine, off)
    send(cross, slot(core), slot(core), mine, off)
    send(near, slot(core), slot(core), mine, on)

    ve.memset(T.one[:, :], 1.0).then_inc(S.fill, 1)
    ve.wait_ge(S.fill, 1)
    ve.tensor_tensor_scan(T.col[:, :], T.one[:, :], T.one[:, :], 0.0, AluOpType.mult, AluOpType.add).then_inc(S.scan, 1)
    ve.wait_ge(S.scan, 1)
    ve.wait_ge(S.tab, len(_peers(twin, T.cores, topo)[3]))
    ve.tensor_scalar(T.eye[:, :], T.col[:, :], T.pr[:, 0:1], None, AluOpType.is_equal).then_inc(S.eye_ok, 1)

    accp = [T.acc_p0, T.acc_p1, T.acc_p2, T.acc_p3]

    def p_part(c, first, last):
        for k in range(4):
            i = te.matmul(accp[k][:, 0:C], slot(c), T.qs[:, k * C:(k + 1) * C], first, last)
            if last:
                i.then_inc(S["mm_p%d" % k], 1)

    def s_part(c, first, last):
        i = te.matmul(T.acc_s[:, 0:D], slot(c), T.eye[:, :], first, last)
        if last:
            i.then_inc(S.mm_s, 1)

    te.wait_ge(S.ld_mt, 16)
    te.wait_ge(S.ld_q, 16)
    p_part(core, True, False)
    te.wait_ge(*landed(twin))
    p_part(twin, False, False)
    te.wait_ge(S.eye_ok, 1)
    s_part(twin, True, False)
    te.wait_ge(*landed(near))
    s_part(near, False, False)
    p_part(near, False, False)
    te.wait_ge(*landed(cross))
    s_part(cross, False, True)
    p_part(cross, False, True)

    ve.wait_ge(S.ld_m, 16)
    ve.wait_ge(S.mm_s, 1)
    ve.tensor_tensor(T.ss[:, :], T.acc_s[:, 0:D], T.ms[:, :], AluOpType.add).then_inc(S.cp_s, 1)
    for k in range(4):
        q = sc if k % 2 == 0 else ve
        q.wait_ge(S["mm_p%d" % k], 1)
        if k % 2 == 0:
            i = sc.activation(T.ps[:, k * C:(k + 1) * C], accp[k][:, 0:C], ActivationFunctionType.Copy)
        else:
            i = ve.tensor_copy(T.ps[:, k * C:(k + 1) * C], accp[k][:, 0:C])
        i.then_inc(S["cp_p%d" % k], 1)

    te.wait_ge(S.cp_s, 1)
    te.wait_ge(S.cp_p0, 1)
    te.wait_ge(S.cp_p1, 1)
    te.matmul(T.acc_qa[:, 0:H], T.ss[:, :], T.ps[:, 0:H], True, True).then_inc(S.mm_qa, 1)
    te.wait_ge(S.cp_p2, 1)
    te.matmul(T.acc_qb[:, 0:C], T.ss[:, :], T.ps[:, H:H + C], True, True).then_inc(S.mm_qb, 1)
    te.wait_ge(S.cp_p3, 1)
    te.matmul(T.acc_qc[:, 0:C], T.ss[:, :], T.ps[:, H + C:R], True, True).then_inc(S.mm_qc, 1)

    ve.wait_ge(S.mm_qa, 1)
    ve.tensor_copy(T.q2s[:, 0:H], T.acc_qa[:, 0:H]).then_inc(S.cp_qa, 1)
    sc.wait_ge(S.mm_qb, 1)
    sc.activation(T.q2s[:, H:H + C], T.acc_qb[:, 0:C], ActivationFunctionType.Copy).then_inc(S.cp_qb, 1)
    sc.wait_ge(S.mm_qc, 1)
    sc.activation(T.q2s[:, H + C:R], T.acc_qc[:, 0:C], ActivationFunctionType.Copy).then_inc(S.cp_qc, 1)

    for k in range(4):
        sy.wait_ge(S["cp_p%d" % k], 1)
    sy.dma_start(T.p[:, :], T.ps[:, :]).then_inc(S.st_p, 16)
    sc.wait_ge(S.cp_qa, 1)
    sc.wait_ge(S.cp_qb, 1)
    sc.wait_ge(S.cp_qc, 1)
    sc.dma_start(T.q2[:, :], T.q2s[:, :]).then_inc(S.st_q, 16)

    g.wait_ge(S.sent, 3 * len(off) + len(on))
    sy.wait_ge(S.st_p, 16)
    sc.wait_ge(S.st_q, 16)
